import numpy as np
import ml_dtypes


def mxq(x, axis, fmt="e4m3"):
    dtype, down = {"e4m3": (ml_dtypes.float8_e4m3fn, 7), "e5m2": (ml_dtypes.float8_e5m2, 14)}[fmt]
    v = np.moveaxis(np.asarray(x, np.float32).astype(ml_dtypes.bfloat16).astype(np.float64), axis, -1)
    blocks = v.reshape(v.shape[:-1] + (-1, 32))
    amax = np.abs(blocks).max(-1, keepdims=True)
    byte = np.maximum(np.where(amax > 0, np.frexp(amax)[1] - 1 + 127, 0) - down, 1)
    scale = np.exp2(byte - 127.0)
    codes = (blocks / scale).astype(np.float32).astype(dtype).astype(np.float64)
    return np.moveaxis((codes * scale).reshape(v.shape), -1, axis)


WIDE = False


def mx_kscale(k):
    if not WIDE:
        return np.ones(k)
    levels = np.array([10, -10, 5, -5, 0])
    if k % 512:
        return np.exp2(np.random.permutation(np.resize(levels, k // 32))).repeat(32)
    a = np.empty((k // 512, 16))
    for p in range(k // 512):
        a[p, :8] = np.random.permutation(np.resize(levels, 8))
        for g in range(8):
            far = levels[np.abs(levels - a[p, g]) >= 10]
            a[p, g + 8] = far[np.random.randint(len(far))]
    return np.exp2(a.ravel()).repeat(32)


def f64(x):
    return np.asarray(x).astype(np.float64)


def striped(idx):
    return np.tile(idx.reshape(-1, 16).T, (8, 1)).astype(np.uint16)


def unstriped(offs):
    return offs[:16].T.reshape(-1).astype(np.int64)


def striped8(idx):
    return np.concatenate([x.reshape(-1, 16).T for x in idx]).astype(np.uint16)


def runs(offs, k):
    lists = np.stack([offs[16 * r : 16 * r + 16].T.reshape(-1) for r in range(8)]).astype(np.int64)
    return lists[np.arange(k) % 512 // 64]


def pack_weight(w):
    k, n = w.shape
    w = f64(np.asarray(w, np.float32).astype(ml_dtypes.bfloat16)).reshape(k // 32, 32, n)
    amax = np.abs(w).max(1)
    byte = np.clip(np.where(amax > 0, np.frexp(amax)[1] - 1 + 127 - 7, 1), 1, 254)
    scaled = (w * np.exp2(127.0 - byte)[:, None, :]).reshape(k, n).astype(np.float32)
    words = np.ascontiguousarray(scaled.reshape(k // 512, 128, 4, n).transpose(0, 1, 3, 2)).astype(ml_dtypes.float8_e4m3fn).view(np.uint8)
    return words, np.ascontiguousarray(byte.astype(np.uint8).reshape(k // 512, 16, n))


def unpack_weight(words, scales):
    g, p, n, _ = words.shape
    vals = np.ascontiguousarray(words).view(ml_dtypes.float8_e4m3fn).astype(np.float64) * np.repeat(np.exp2(scales.astype(np.float64) - 127.0), 8, axis=1)[..., None]
    return vals.transpose(0, 1, 3, 2).reshape(g * 512, n)


E2M1 = np.array([0.0, 0.5, 1.0, 1.5, 2.0, 3.0, 4.0, 6.0, -0.0, -0.5, -1.0, -1.5, -2.0, -3.0, -4.0, -6.0])


def pack_fp4(w):
    k, n = w.shape
    w = f64(np.asarray(w, np.float32).astype(ml_dtypes.bfloat16)).reshape(k // 32, 32, n)
    amax = np.abs(w).max(1)
    mant, ex = np.frexp(amax / 6.0)
    byte = np.clip(np.where(amax > 0, np.where(mant > 0.5, ex, ex - 1) + 127, 1), 1, 254)
    scaled = (w * np.exp2(127.0 - byte)[:, None, :]).reshape(k, n).astype(np.float32)
    c = np.ascontiguousarray(scaled.reshape(k // 512, 128, 4, n).transpose(0, 1, 3, 2)).astype(ml_dtypes.float4_e2m1fn).view(np.uint8) & 0xF
    words = (c[..., 0::2] | (c[..., 1::2] << 4)).reshape(k // 512, 128, 2 * n)
    return np.ascontiguousarray(words), np.ascontiguousarray(byte.astype(np.uint8).reshape(k // 512, 16, n))


def unpack_fp4(words, scales):
    g, _, n = scales.shape
    words = np.ascontiguousarray(words).reshape(g, 128, n, 2)
    nib = np.empty((g, 128, n, 4), np.uint8)
    nib[..., 0::2] = words & 0xF
    nib[..., 1::2] = words >> 4
    vals = E2M1[nib] * np.repeat(np.exp2(scales.astype(np.float64) - 127.0), 8, axis=1)[..., None]
    return vals.transpose(0, 1, 3, 2).reshape(g * 512, n)


def planes(y):
    n, m = y.shape
    v = y.astype(np.float32).astype(ml_dtypes.bfloat16).astype(np.float64).reshape(n // 32, 32, m)
    top = np.abs(v).max(1)
    byte = np.clip(np.where(top > 0, np.frexp(top)[1] - 1 + 127 - 7, 1), 1, 254)
    codes = (v * np.exp2(127.0 - byte)[:, None, :]).reshape(n, m).astype(np.float32).astype(ml_dtypes.float8_e4m3fn).view(np.uint8)
    words = codes.reshape(n // 512, 128, 4, m).transpose(0, 1, 3, 2)
    return np.ascontiguousarray(words), np.ascontiguousarray(byte.astype(np.uint8).reshape(n // 512, 16, m))


K, T, S, N, H, W = 512, 2048, 512, 512, 512, 2048


def setup_inputs():
    n = np.random.standard_normal
    s = mx_kscale(K)[:, None]
    u = mx_kscale(H)
    packed_xT = pack_weight(n((K, T)) * s)
    packed_w1 = pack_fp4(n((K, H)) / np.sqrt(K) / s)
    packed_w2 = pack_fp4(n((H, N)) / np.sqrt(2 * H) / u[:, None])
    packed_w3 = pack_fp4(n((K, N)) / np.sqrt(2 * K) / s)
    return {
        "x_words": packed_xT[0],
        "x_scales": packed_xT[1],
        "w1_words": packed_w1[0],
        "w1_scales": packed_w1[1],
        "gn": (np.random.uniform(0.5, 1.5, (H, 1)) * u[:, None]).astype(np.float32),
        "w2_words": packed_w2[0],
        "w2_scales": packed_w2[1],
        "w3_words": packed_w3[0],
        "w3_scales": packed_w3[1],
        "tau": np.random.uniform(0.3, 0.9, (N, 1)).astype(np.float32),
        "offs": striped(np.random.permutation(T)[:S]),
        "n1": striped(np.random.permutation(S)),
        "n2": striped(np.random.permutation(S)),
        "n3": striped(np.random.permutation(S)),
        "hz": striped8(np.random.randint(0, T, (8, S))),
        "n4": striped(np.random.randint(0, S, W)),
    }


def reference(x_words, x_scales, w1_words, w1_scales, gn, w2_words, w2_scales, w3_words, w3_scales, tau, offs, n1, n2, n3, hz, n4):
    xq = unpack_weight(x_words, x_scales)[:, unstriped(offs)]
    y = unpack_fp4(w1_words, w1_scales).T @ xq
    ex = np.exp(0.5 * y)
    z = f64(gn) * (np.log((ex + ex[:, unstriped(n1)]) / (ex[:, unstriped(n2)] + ex[:, unstriped(n3)])))
    x_hz = unpack_weight(x_words, x_scales)[np.arange(K)[:, None], runs(hz, K)]
    h = unpack_fp4(w2_words, w2_scales).T @ mxq(z, 0, "e4m3") + unpack_fp4(w3_words, w3_scales).T @ x_hz
    top = h.max(axis=1, keepdims=True)
    ea = np.exp(f64(tau) * (h[:, unstriped(n4)] - top))
    ms = ea.reshape(N, S, 4).sum(axis=2)
    out_0 = np.log(ms + 0.25) - (0.5 * h)
    return (out_0,) + planes(out_0)

@@ -1,0 +1,225 @@
+from contextlib import ExitStack
+
+import concourse.mybir as mybir
+
+K, T, S, N, H, W = 512, 2048, 512, 512, 512, 2048
+FLOPS = 3 * 2 * 512 * 512 * 512
+
+F32 = mybir.dt.float32
+BF16 = mybir.dt.bfloat16
+I32 = mybir.dt.int32
+U32 = mybir.dt.uint32
+U16 = mybir.dt.uint16
+U8 = mybir.dt.uint8
+FP8X4 = mybir.dt.float8_e4m3fn_x4
+FP4X4 = mybir.dt.float4_e2m1fn_x4
+ACT = mybir.ActivationFunctionType
+ALU = mybir.AluOpType
+AX = mybir.AxisListType
+
+P = 128
+PACK = 4
+HALF = S // 2
+CH = 128
+NCH = S // CH
+MEMBERS = 4
+
+
+def tile_picked_mixhoddsegl_none_po_kernel(
+    tc, x_words, x_scales, w1_words, w1_scales, gn, w2_words, w2_scales, w3_words, w3_scales, tau,
+    offs, n1, n2, n3, hz, n4, out_0, out_1, out_2,
+):
+    nc = tc.nc
+    with ExitStack() as ctx:
+        lists = ctx.enter_context(tc.tile_pool(name="lists", bufs=1))
+        keep = ctx.enter_context(tc.tile_pool(name="keep", bufs=1))
+        psum = ctx.enter_context(tc.psum_pool(name="psum", bufs=1))
+
+        def sb(shape, dtype, name):
+            return keep.tile(shape, dtype, name=name, align_bytes=64)
+
+        def load_list(src, name):
+            t = lists.tile(list(src.shape), U16, name=name)
+            nc.sync.dma_start(t[:], src)
+            return t
+
+        def load_scale_quadrant(src, q):
+            nc.sync.dma_start(ws_raw[32 * q : 32 * q + 4, :].bitcast(I32), src[0, 4 * q : 4 * q + 4, :].bitcast(I32))
+
+        def load_weight(words, scales):
+            nc.sync.dma_start(w_raw[:].bitcast(I32), words[0].bitcast(I32))
+            for q in range(4):
+                load_scale_quadrant(scales, q)
+
+        w_raw = sb([P, 2 * N], U8, "w_raw")
+        ws_raw = sb([P, N], U8, "ws_raw")
+
+        def deal_scales(name):
+            t = sb([P, N], U8, name)
+            nc.vector.tensor_copy(
+                t[:].rearrange("p (t m) -> p t m", t=PACK), ws_raw[:].rearrange("p (m t) -> p t m", t=PACK)
+            )
+            return t
+
+        def deal_words(name):
+            t = sb([P, 2 * N], U8, name)
+            nc.vector.tensor_copy(
+                t[:].rearrange("p (t m b) -> p t m b", t=PACK, b=2),
+                w_raw[:].rearrange("p (m t b) -> p t m b", t=PACK, b=2),
+            )
+            return t
+
+        xs = sb([P, T], U8, "xs")
+        nc.vector.memset(xs[:].bitcast(I32), 0)
+        nc.vector.memset(ws_raw[:].bitcast(I32), 0)
+        offs_t = load_list(offs, "offs_t")
+        nc.sync.dma_start(w_raw[:].bitcast(I32), w1_words[0].bitcast(I32))
+        xs_rows = x_scales[0].bitcast(I32).rearrange("(q r) w -> r q w", r=4)
+        for r in range(2):
+            nc.sync.dma_start(xs[r:P:32, :].bitcast(I32), xs_rows[r])
+        for r in range(2, 4):
+            nc.sync.dma_start(xs[r:P:16, :].bitcast(I32), xs_rows[r].unsqueeze(1).to_broadcast([4, 2, T // 4]))
+        load_scale_quadrant(w1_scales, 0)
+        xw = sb([P, T], U32, "xw")
+        nc.sync.dma_start(xw[:].bitcast(I32), x_words[0].rearrange("p n t -> p (n t)").bitcast(I32))
+        for q in range(1, 4):
+            load_scale_quadrant(w1_scales, q)
+
+        hzs = sb([P, S], U8, "hzs")
+        nc.vector.memset(hzs[:].bitcast(I32), 0)
+        quarter = sb([P, 1], F32, "quarter")
+        nc.vector.memset(quarter[:], 0.25)
+        hw = [sb([P, 2 * S], F32, "hw%d" % t) for t in range(PACK)]
+        for t in range(PACK):
+            nc.vector.memset(hw[t][:, S:], 0.0)
+
+        hz_t = load_list(hz, "hz_t")
+        n1_t = load_list(n1, "n1_t")
+        n3_t = load_list(n3, "n3_t")
+        n2_t = load_list(n2, "n2_t")
+        n4_t = load_list(n4, "n4_t")
+        gn_t = sb([P, PACK], F32, "gn_t")
+        nc.sync.dma_start(gn_t[:], gn.rearrange("(p t) o -> p (t o)", t=PACK))
+        tau_t = sb([P, PACK], F32, "tau_t")
+        nc.sync.dma_start(tau_t[:], tau.rearrange("(p t) o -> p (t o)", t=PACK))
+
+        w1 = sb([P, 2 * N], U8, "w1")
+        nc.scalar.copy(
+            w1[:].bitcast(U16).rearrange("p (t m) -> p t m", t=PACK),
+            w_raw[:].bitcast(U16).rearrange("p (m t) -> p t m", t=PACK),
+        )
+        w1s = deal_scales("w1s")
+
+        def product(out, w, ws, t, codes, scales, start, stop):
+            nc.tensor.matmul_mx(
+                out=out,
+                lhsT=w[:, 2 * P * t : 2 * P * (t + 1)].bitcast(FP4X4),
+                lhsT_scale=ws[:, P * t : P * (t + 1)],
+                rhs=codes.bitcast(FP8X4),
+                rhs_scale=scales,
+                start=start,
+                stop=stop,
+            )
+
+        xq_s = sb([P, S], U8, "xq_s")
+        nc.vector.tensor_copy(xq_s[:], xs[:].indirect(offs_t[:]))
+        ex = [sb([P, S], F32, "ex%d" % t) for t in range(PACK)]
+        for u in range(2):
+            cols = slice(HALF * u, HALF * (u + 1))
+            xq_w = sb([P, HALF], U32, "xq_w%d" % u)
+            nc.vector.tensor_copy(xq_w[:], xw[:].indirect(offs_t[:, 16 * u : 16 * (u + 1)]))
+            for t in range(PACK):
+                y = psum.tile([P, HALF], F32, name="y%d_%d" % (u, t), tag="bank%d" % (4 * u + t))
+                product(y[:], w1, w1s, t, xq_w[:], xq_s[:, cols], True, True)
+                nc.scalar.activation(ex[t][:, cols], y[:], ACT.Exp, scale=0.5)
+
+        hz_w = sb([P, S], U32, "hz_w")
+        nc.vector.tensor_copy(hz_w[:], xw[:].indirect(hz_t[:]))
+        hz_s_raw = sb([P, S], U8, "hz_s_raw")
+        nc.vector.tensor_copy(hz_s_raw[:], xs[:].indirect(hz_t[:]))
+        for r in range(4):
+            first = r if r < 2 else 16 + r
+            nc.sync.dma_start(hzs[r:P:32, :].bitcast(I32), hz_s_raw[first:P:32, :].bitcast(I32))
+        load_weight(w3_words, w3_scales)
+        w3 = deal_words("w3")
+        w3s = deal_scales("w3s")
+        load_weight(w2_words, w2_scales)
+        w2 = deal_words("w2")
+        w2s = deal_scales("w2s")
+
+        h_ps = [psum.tile([P, S], F32, name="h%d" % t, tag="bank%d" % t) for t in range(PACK)]
+        nd = [sb([P, 2, PACK, CH], F32, "nd%d" % c) for c in range(NCH)]
+
+        def fetch(c):
+            cols = slice(CH * c, CH * (c + 1))
+            lc = slice(CH // 16 * c, CH // 16 * (c + 1))
+            for t in range(PACK):
+                g1 = sb([P, CH], F32, "g1_%d_%d" % (c, t))
+                nc.scalar.activation(g1[:], ex[t][:].indirect(n1_t[:, lc]), ACT.Copy)
+                g3 = sb([P, CH], F32, "g3_%d_%d" % (c, t))
+                nc.scalar.activation(g3[:], ex[t][:].indirect(n3_t[:, lc]), ACT.Copy)
+                nc.vector.tensor_tensor(nd[c][:, 0, t, :], ex[t][:, cols], g1[:], ALU.add)
+                nc.vector.tensor_tensor(nd[c][:, 1, t, :], ex[t][:].indirect(n2_t[:, lc]), g3[:], ALU.add)
+
+        def second(c):
+            cols = slice(CH * c, CH * (c + 1))
+            lg = sb([P, 2, PACK, CH], F32, "lg%d" % c)
+            nc.scalar.activation(lg[:], nd[c][:], ACT.Ln)
+            diff = sb([P, PACK, CH], F32, "diff%d" % c)
+            nc.vector.tensor_tensor(diff[:], lg[:, 0], lg[:, 1], ALU.subtract)
+            z = sb([P, CH, PACK], BF16, "z%d" % c)
+            nc.vector.tensor_tensor(
+                z[:], diff[:].rearrange("p t j -> p j t"), gn_t[:].unsqueeze(1).to_broadcast([P, CH, PACK]), ALU.mult
+            )
+            z_w = sb([P, CH], U32, "z_w%d" % c)
+            z_s = sb([P, CH], U8, "z_s%d" % c)
+            nc.vector.quantize_mx(out=z_w[:].bitcast(FP8X4), scales=z_s[:], in_=z[:].rearrange("p j t -> p (j t)"))
+            for t in range(PACK):
+                product(h_ps[t][:, cols], w3, w3s, t, hz_w[:, cols], hzs[:, cols], True, False)
+                product(h_ps[t][:, cols], w2, w2s, t, z_w[:], z_s[:], False, True)
+
+        for c in range(NCH + 1):
+            if c < NCH:
+                fetch(c)
+            if c > 0:
+                second(c - 1)
+
+        ms = sb([P, PACK, S], F32, "ms")
+        half_h = sb([P, PACK, S], F32, "half_h")
+        for t in range(PACK):
+            top = sb([P, 1], F32, "top%d" % t)
+            nc.vector.tensor_scalar(hw[t][:, :S], h_ps[t][:], 1.0, None, ALU.mult, ALU.max, accum_out=top[:])
+            shift = sb([P, 1], F32, "shift%d" % t)
+            nc.vector.tensor_scalar(shift[:], top[:], tau_t[:, t : t + 1], -1.0, ALU.mult, ALU.mult)
+            for c in range(NCH):
+                ea = sb([P, CH, MEMBERS], F32, "ea%d_%d" % (t, c))
+                nc.scalar.activation(
+                    ea[:].rearrange("p j m -> p (j m)"),
+                    hw[t][:].indirect(n4_t[:, 32 * c : 32 * (c + 1)]),
+                    ACT.Exp,
+                    bias=shift[:],
+                    scale=tau_t[:, t : t + 1],
+                )
+                nc.vector.tensor_reduce(ms[:, t, CH * c : CH * (c + 1)], ea[:], AX.X, ALU.add)
+            nc.vector.tensor_scalar(half_h[:, t, :], hw[t][:, :S], -0.5, None, ALU.mult)
+
+        out_rows = out_0.rearrange("(p t) j -> p t j", t=PACK)
+        out_words = out_1[0].rearrange("p n t -> p (n t)").bitcast(I32)
+        o_w = sb([P, S], U32, "o_w")
+        o_s = sb([P, S], U8, "o_s")
+        for c in range(NCH):
+            cols = slice(CH * c, CH * (c + 1))
+            lm = sb([P, PACK, CH], F32, "lm%d" % c)
+            nc.scalar.activation(lm[:], ms[:, :, cols], ACT.Ln, bias=quarter[:])
+            res = sb([P, PACK, CH], F32, "res%d" % c)
+            nc.vector.tensor_tensor(res[:], lm[:], half_h[:, :, cols], ALU.add)
+            nc.sync.dma_start(out_rows[:, :, cols], res[:])
+            rb = sb([P, CH, PACK], BF16, "rb%d" % c)
+            nc.vector.tensor_copy(rb[:], res[:].rearrange("p t j -> p j t"))
+            nc.vector.quantize_mx(
+                out=o_w[:, cols].bitcast(FP8X4), scales=o_s[:, cols], in_=rb[:].rearrange("p j t -> p (j t)")
+            )
+            nc.sync.dma_start(out_words[:, cols], o_w[:, cols].bitcast(I32))
+        for q in range(4):
+            queue = nc.sync if q % 2 == 0 else nc.scalar
+            queue.dma_start(out_2[0, 4 * q : 4 * q + 4, :].bitcast(I32), o_s[32 * q : 32 * q + 4, :].bitcast(I32))

@@ -43,63 +43,48 @@ def tile_picked_mixhoddsegl_none_po_kernel(
             nc.sync.dma_start(t[:], src)
             return t
 
-        def load_scale_quadrant(src, q):
-            nc.sync.dma_start(ws_raw[32 * q : 32 * q + 4, :].bitcast(I32), src[0, 4 * q : 4 * q + 4, :].bitcast(I32))
-
-        def load_weight(words, scales):
-            nc.sync.dma_start(w_raw[:].bitcast(I32), words[0].bitcast(I32))
-            for q in range(4):
-                load_scale_quadrant(scales, q)
+        def load_scale_quadrant(queue, dst, src, q):
+            queue.dma_start(dst[32 * q : 32 * q + 4, :].bitcast(I32), src[0, 4 * q : 4 * q + 4, :].bitcast(I32))
 
         w_raw = sb([P, 2 * N], U8, "w_raw")
         ws_raw = sb([P, N], U8, "ws_raw")
-
-        def deal_scales(name):
-            t = sb([P, N], U8, name)
-            nc.vector.tensor_copy(
-                t[:].rearrange("p (t m) -> p t m", t=PACK), ws_raw[:].rearrange("p (m t) -> p t m", t=PACK)
-            )
-            return t
-
-        def deal_words(name):
-            t = sb([P, 2 * N], U8, name)
-            nc.vector.tensor_copy(
-                t[:].rearrange("p (t m b) -> p t m b", t=PACK, b=2),
-                w_raw[:].rearrange("p (m t b) -> p t m b", t=PACK, b=2),
-            )
-            return t
+        v_raw = sb([P, 2, 2 * N], U8, "v_raw")
+        vs_raw = sb([P, 2, N], U8, "vs_raw")
 
         xs = sb([P, T], U8, "xs")
         nc.vector.memset(xs[:].bitcast(I32), 0)
         nc.vector.memset(ws_raw[:].bitcast(I32), 0)
         offs_t = load_list(offs, "offs_t")
-        nc.sync.dma_start(w_raw[:].bitcast(I32), w1_words[0].bitcast(I32))
-        xs_rows = x_scales[0].bitcast(I32).rearrange("(q r) w -> r q w", r=4)
-        for r in range(2):
-            nc.sync.dma_start(xs[r:P:32, :].bitcast(I32), xs_rows[r])
-        for r in range(2, 4):
-            nc.sync.dma_start(xs[r:P:16, :].bitcast(I32), xs_rows[r].unsqueeze(1).to_broadcast([4, 2, T // 4]))
-        load_scale_quadrant(w1_scales, 0)
+        nc.gpsimd.dma_start(w_raw[:].bitcast(I32), w1_words[0].bitcast(I32))
+        for q in range(4):
+            load_scale_quadrant(nc.sync if q < 2 else nc.gpsimd, ws_raw, w1_scales, q)
         xw = sb([P, T], U32, "xw")
         nc.sync.dma_start(xw[:].bitcast(I32), x_words[0].rearrange("p n t -> p (n t)").bitcast(I32))
-        for q in range(1, 4):
-            load_scale_quadrant(w1_scales, q)
+        xs_rows = x_scales[0].bitcast(I32).rearrange("(q r) w -> r q w", r=4)
+        for r in range(2):
+            nc.scalar.dma_start(xs[r:P:32, :].bitcast(I32), xs_rows[r])
+        for r in range(2, 4):
+            nc.scalar.dma_start(xs[r:P:16, :].bitcast(I32), xs_rows[r].unsqueeze(1).to_broadcast([4, 2, T // 4]))
 
+        nc.vector.memset(vs_raw[:].rearrange("p i n -> p (i n)").bitcast(I32), 0)
         hzs = sb([P, S], U8, "hzs")
         nc.vector.memset(hzs[:].bitcast(I32), 0)
         quarter = sb([P, 1], F32, "quarter")
         nc.vector.memset(quarter[:], 0.25)
-        hw = [sb([P, 2 * S], F32, "hw%d" % t) for t in range(PACK)]
-        for t in range(PACK):
-            nc.vector.memset(hw[t][:, S:], 0.0)
+        hw = [sb([P, 4 * S], F32, "hw%d" % t) for t in range(PACK)]
 
-        hz_t = load_list(hz, "hz_t")
         n1_t = load_list(n1, "n1_t")
         n3_t = load_list(n3, "n3_t")
         n2_t = load_list(n2, "n2_t")
         n4_t = load_list(n4, "n4_t")
+        for i, words in enumerate((w2_words, w3_words)):
+            nc.sync.dma_start(v_raw[:, i, :].bitcast(I32), words[0].bitcast(I32))
+        hz_t = load_list(hz, "hz_t")
         gn_t = sb([P, PACK], F32, "gn_t")
         nc.sync.dma_start(gn_t[:], gn.rearrange("(p t) o -> p (t o)", t=PACK))
+        for i, scales in enumerate((w2_scales, w3_scales)):
+            for q in range(4):
+                load_scale_quadrant(nc.sync, vs_raw[:, i, :], scales, q)
         tau_t = sb([P, PACK], F32, "tau_t")
         nc.sync.dma_start(tau_t[:], tau.rearrange("(p t) o -> p (t o)", t=PACK))
 
@@ -108,7 +93,10 @@ def tile_picked_mixhoddsegl_none_po_kernel(
             w1[:].bitcast(U16).rearrange("p (t m) -> p t m", t=PACK),
             w_raw[:].bitcast(U16).rearrange("p (m t) -> p t m", t=PACK),
         )
-        w1s = deal_scales("w1s")
+        w1s = sb([P, N], U8, "w1s")
+        nc.vector.tensor_copy(
+            w1s[:].rearrange("p (t m) -> p t m", t=PACK), ws_raw[:].rearrange("p (m t) -> p t m", t=PACK)
+        )
 
         def product(out, w, ws, t, codes, scales, start, stop):
             nc.tensor.matmul_mx(
@@ -140,36 +128,40 @@ def tile_picked_mixhoddsegl_none_po_kernel(
         for r in range(4):
             first = r if r < 2 else 16 + r
             nc.sync.dma_start(hzs[r:P:32, :].bitcast(I32), hz_s_raw[first:P:32, :].bitcast(I32))
-        load_weight(w3_words, w3_scales)
-        w3 = deal_words("w3")
-        w3s = deal_scales("w3s")
-        load_weight(w2_words, w2_scales)
-        w2 = deal_words("w2")
-        w2s = deal_scales("w2s")
+        v = sb([P, 2, 2 * N], U8, "v")
+        nc.vector.tensor_copy(
+            v[:].rearrange("p i (t m b) -> p i t m b", t=PACK, b=2),
+            v_raw[:].rearrange("p i (m t b) -> p i t m b", t=PACK, b=2),
+        )
+        vs = sb([P, 2, N], U8, "vs")
+        nc.vector.tensor_copy(
+            vs[:].rearrange("p i (t m) -> p i t m", t=PACK), vs_raw[:].rearrange("p i (m t) -> p i t m", t=PACK)
+        )
+        w2, w2s, w3, w3s = v[:, 0, :], vs[:, 0, :], v[:, 1, :], vs[:, 1, :]
 
         h_ps = [psum.tile([P, S], F32, name="h%d" % t, tag="bank%d" % t) for t in range(PACK)]
-        nd = [sb([P, 2, PACK, CH], F32, "nd%d" % c) for c in range(NCH)]
+        ring = [sb([P, 2, PACK, CH], F32, "ring%d" % i) for i in range(3)]
+        fetched = [ring[2 * c % 3] for c in range(NCH)]
+        nd = [ring[(2 * c + 1) % 3] for c in range(NCH)]
 
         def fetch(c):
             cols = slice(CH * c, CH * (c + 1))
             lc = slice(CH // 16 * c, CH // 16 * (c + 1))
             for t in range(PACK):
-                g1 = sb([P, CH], F32, "g1_%d_%d" % (c, t))
-                nc.scalar.activation(g1[:], ex[t][:].indirect(n1_t[:, lc]), ACT.Copy)
-                g3 = sb([P, CH], F32, "g3_%d_%d" % (c, t))
-                nc.scalar.activation(g3[:], ex[t][:].indirect(n3_t[:, lc]), ACT.Copy)
-                nc.vector.tensor_tensor(nd[c][:, 0, t, :], ex[t][:, cols], g1[:], ALU.add)
-                nc.vector.tensor_tensor(nd[c][:, 1, t, :], ex[t][:].indirect(n2_t[:, lc]), g3[:], ALU.add)
+                g1, g3 = fetched[c][:, 0, t, :], fetched[c][:, 1, t, :]
+                nc.scalar.activation(g1, ex[t][:].indirect(n1_t[:, lc]), ACT.Copy)
+                nc.scalar.activation(g3, ex[t][:].indirect(n3_t[:, lc]), ACT.Copy)
+                nc.vector.tensor_tensor(nd[c][:, 0, t, :], ex[t][:, cols], g1, ALU.add)
+                nc.vector.tensor_tensor(nd[c][:, 1, t, :], ex[t][:].indirect(n2_t[:, lc]), g3, ALU.add)
 
         def second(c):
             cols = slice(CH * c, CH * (c + 1))
-            lg = sb([P, 2, PACK, CH], F32, "lg%d" % c)
-            nc.scalar.activation(lg[:], nd[c][:], ACT.Ln)
-            diff = sb([P, PACK, CH], F32, "diff%d" % c)
-            nc.vector.tensor_tensor(diff[:], lg[:, 0], lg[:, 1], ALU.subtract)
+            diff, lg = hw[c][:, S : 2 * S], hw[c][:, 2 * S :]
+            nc.scalar.activation(lg, nd[c][:].rearrange("p s t j -> p (s t j)"), ACT.Ln)
+            nc.vector.tensor_tensor(diff, lg[:, :S], lg[:, S:], ALU.subtract)
             z = sb([P, CH, PACK], BF16, "z%d" % c)
             nc.vector.tensor_tensor(
-                z[:], diff[:].rearrange("p t j -> p j t"), gn_t[:].unsqueeze(1).to_broadcast([P, CH, PACK]), ALU.mult
+                z[:], diff.rearrange("p (t j) -> p j t", t=PACK), gn_t[:].unsqueeze(1).to_broadcast([P, CH, PACK]), ALU.mult
             )
             z_w = sb([P, CH], U32, "z_w%d" % c)
             z_s = sb([P, CH], U8, "z_s%d" % c)
@@ -191,16 +183,16 @@ def tile_picked_mixhoddsegl_none_po_kernel(
             nc.vector.tensor_scalar(hw[t][:, :S], h_ps[t][:], 1.0, None, ALU.mult, ALU.max, accum_out=top[:])
             shift = sb([P, 1], F32, "shift%d" % t)
             nc.vector.tensor_scalar(shift[:], top[:], tau_t[:, t : t + 1], -1.0, ALU.mult, ALU.mult)
-            for c in range(NCH):
-                ea = sb([P, CH, MEMBERS], F32, "ea%d_%d" % (t, c))
+            for c in range(2):
+                ea = sb([P, HALF, MEMBERS], F32, "ea%d_%d" % (t, c))
                 nc.scalar.activation(
                     ea[:].rearrange("p j m -> p (j m)"),
-                    hw[t][:].indirect(n4_t[:, 32 * c : 32 * (c + 1)]),
+                    hw[t][:].indirect(n4_t[:, 64 * c : 64 * (c + 1)]),
                     ACT.Exp,
                     bias=shift[:],
                     scale=tau_t[:, t : t + 1],
                 )
-                nc.vector.tensor_reduce(ms[:, t, CH * c : CH * (c + 1)], ea[:], AX.X, ALU.add)
+                nc.vector.tensor_reduce(ms[:, t, HALF * c : HALF * (c + 1)], ea[:], AX.X, ALU.add)
             nc.vector.tensor_scalar(half_h[:, t, :], hw[t][:, :S], -0.5, None, ALU.mult)
 
         out_rows = out_0.rearrange("(p t) j -> p t j", t=PACK)
@@ -215,7 +207,10 @@ def tile_picked_mixhoddsegl_none_po_kernel(
             nc.vector.tensor_tensor(res[:], lm[:], half_h[:, :, cols], ALU.add)
             nc.sync.dma_start(out_rows[:, :, cols], res[:])
             rb = sb([P, CH, PACK], BF16, "rb%d" % c)
-            nc.vector.tensor_copy(rb[:], res[:].rearrange("p t j -> p j t"))
+            if c in (1, 2):
+                nc.scalar.copy(rb[:], res[:].rearrange("p t j -> p j t"))
+            else:
+                nc.vector.tensor_copy(rb[:], res[:].rearrange("p t j -> p j t"))
             nc.vector.quantize_mx(
                 out=o_w[:, cols].bitcast(FP8X4), scales=o_s[:, cols], in_=rb[:].rearrange("p j t -> p (j t)")
             )

@@ -52,19 +52,20 @@ def tile_picked_mixhoddsegl_none_po_kernel(
         vs_raw = sb([P, 2, N], U8, "vs_raw")
 
         xs = sb([P, T], U8, "xs")
-        nc.vector.memset(xs[:].bitcast(I32), 0)
+        nc.gpsimd.memset(xs[:].bitcast(I32), 0)
         nc.vector.memset(ws_raw[:].bitcast(I32), 0)
         offs_t = load_list(offs, "offs_t")
-        nc.gpsimd.dma_start(w_raw[:].bitcast(I32), w1_words[0].bitcast(I32))
-        for q in range(4):
-            load_scale_quadrant(nc.sync if q < 2 else nc.gpsimd, ws_raw, w1_scales, q)
-        xw = sb([P, T], U32, "xw")
-        nc.sync.dma_start(xw[:].bitcast(I32), x_words[0].rearrange("p n t -> p (n t)").bitcast(I32))
+        nc.sync.dma_start(w_raw[:].bitcast(I32), w1_words[0].bitcast(I32))
         xs_rows = x_scales[0].bitcast(I32).rearrange("(q r) w -> r q w", r=4)
         for r in range(2):
-            nc.scalar.dma_start(xs[r:P:32, :].bitcast(I32), xs_rows[r])
+            nc.sync.dma_start(xs[r:P:32, :].bitcast(I32), xs_rows[r])
         for r in range(2, 4):
-            nc.scalar.dma_start(xs[r:P:16, :].bitcast(I32), xs_rows[r].unsqueeze(1).to_broadcast([4, 2, T // 4]))
+            nc.sync.dma_start(xs[r:P:16, :].bitcast(I32), xs_rows[r].unsqueeze(1).to_broadcast([4, 2, T // 4]))
+        load_scale_quadrant(nc.sync, ws_raw, w1_scales, 0)
+        xw = sb([P, T], U32, "xw")
+        nc.sync.dma_start(xw[:].bitcast(I32), x_words[0].rearrange("p n t -> p (n t)").bitcast(I32))
+        for q in range(1, 4):
+            load_scale_quadrant(nc.sync, ws_raw, w1_scales, q)
 
         nc.vector.memset(vs_raw[:].rearrange("p i n -> p (i n)").bitcast(I32), 0)
         hzs = sb([P, S], U8, "hzs")
@@ -73,20 +74,17 @@ def tile_picked_mixhoddsegl_none_po_kernel(
         nc.vector.memset(quarter[:], 0.25)
         hw = [sb([P, 4 * S], F32, "hw%d" % t) for t in range(PACK)]
 
+        hz_t = load_list(hz, "hz_t")
         n1_t = load_list(n1, "n1_t")
         n3_t = load_list(n3, "n3_t")
         n2_t = load_list(n2, "n2_t")
-        n4_t = load_list(n4, "n4_t")
-        for i, words in enumerate((w2_words, w3_words)):
-            nc.sync.dma_start(v_raw[:, i, :].bitcast(I32), words[0].bitcast(I32))
-        hz_t = load_list(hz, "hz_t")
         gn_t = sb([P, PACK], F32, "gn_t")
         nc.sync.dma_start(gn_t[:], gn.rearrange("(p t) o -> p (t o)", t=PACK))
+        for i, words in enumerate((w2_words, w3_words)):
+            nc.sync.dma_start(v_raw[:, i, :].bitcast(I32), words[0].bitcast(I32))
         for i, scales in enumerate((w2_scales, w3_scales)):
             for q in range(4):
                 load_scale_quadrant(nc.sync, vs_raw[:, i, :], scales, q)
-        tau_t = sb([P, PACK], F32, "tau_t")
-        nc.sync.dma_start(tau_t[:], tau.rearrange("(p t) o -> p (t o)", t=PACK))
 
         w1 = sb([P, 2 * N], U8, "w1")
         nc.scalar.copy(
@@ -94,7 +92,7 @@ def tile_picked_mixhoddsegl_none_po_kernel(
             w_raw[:].bitcast(U16).rearrange("p (m t) -> p t m", t=PACK),
         )
         w1s = sb([P, N], U8, "w1s")
-        nc.vector.tensor_copy(
+        nc.gpsimd.tensor_copy(
             w1s[:].rearrange("p (t m) -> p t m", t=PACK), ws_raw[:].rearrange("p (m t) -> p t m", t=PACK)
         )
 
@@ -128,11 +126,15 @@ def tile_picked_mixhoddsegl_none_po_kernel(
         for r in range(4):
             first = r if r < 2 else 16 + r
             nc.sync.dma_start(hzs[r:P:32, :].bitcast(I32), hz_s_raw[first:P:32, :].bitcast(I32))
+        n4_t = load_list(n4, "n4_t")
+        tau_t = sb([P, PACK], F32, "tau_t")
+        nc.sync.dma_start(tau_t[:], tau.rearrange("(p t) o -> p (t o)", t=PACK))
         v = sb([P, 2, 2 * N], U8, "v")
-        nc.vector.tensor_copy(
-            v[:].rearrange("p i (t m b) -> p i t m b", t=PACK, b=2),
-            v_raw[:].rearrange("p i (m t b) -> p i t m b", t=PACK, b=2),
-        )
+        for i in range(2):
+            nc.gpsimd.tensor_copy(
+                v[:, i, :].rearrange("p (t m b) -> p t m b", t=PACK, b=2),
+                v_raw[:, i, :].rearrange("p (m t b) -> p t m b", t=PACK, b=2),
+            )
         vs = sb([P, 2, N], U8, "vs")
         nc.vector.tensor_copy(
             vs[:].rearrange("p i (t m) -> p i t m", t=PACK), vs_raw[:].rearrange("p i (m t) -> p i t m", t=PACK)
@@ -140,29 +142,37 @@ def tile_picked_mixhoddsegl_none_po_kernel(
         w2, w2s, w3, w3s = v[:, 0, :], vs[:, 0, :], v[:, 1, :], vs[:, 1, :]
 
         h_ps = [psum.tile([P, S], F32, name="h%d" % t, tag="bank%d" % t) for t in range(PACK)]
-        ring = [sb([P, 2, PACK, CH], F32, "ring%d" % i) for i in range(3)]
-        fetched = [ring[2 * c % 3] for c in range(NCH)]
-        nd = [ring[(2 * c + 1) % 3] for c in range(NCH)]
+        nd = [sb([P, 2, PACK, CH], F32, "nd%d" % c) for c in range(NCH)]
+        first = [sb([P, PACK, CH], F32, "first%d" % i) for i in range(3)]
+        spaces = [f[:] for f in first] + [nd[c][:, s] for c in range(NCH) for s in range(2)]
 
-        def fetch(c):
-            cols = slice(CH * c, CH * (c + 1))
+        def fetch(c, t):
             lc = slice(CH // 16 * c, CH // 16 * (c + 1))
-            for t in range(PACK):
-                g1, g3 = fetched[c][:, 0, t, :], fetched[c][:, 1, t, :]
-                nc.scalar.activation(g1, ex[t][:].indirect(n1_t[:, lc]), ACT.Copy)
-                nc.scalar.activation(g3, ex[t][:].indirect(n3_t[:, lc]), ACT.Copy)
-                nc.vector.tensor_tensor(nd[c][:, 0, t, :], ex[t][:, cols], g1, ALU.add)
-                nc.vector.tensor_tensor(nd[c][:, 1, t, :], ex[t][:].indirect(n2_t[:, lc]), g3, ALU.add)
+            space = spaces[2 * c + t // 2]
+            g1, g3 = space[:, 2 * (t % 2), :], space[:, 2 * (t % 2) + 1, :]
+            nc.scalar.activation(g1, ex[t][:].indirect(n1_t[:, lc]), ACT.Copy)
+            nc.scalar.activation(g3, ex[t][:].indirect(n3_t[:, lc]), ACT.Copy)
+            nc.vector.tensor_tensor(nd[c][:, 0, t, :], ex[t][:, CH * c : CH * (c + 1)], g1, ALU.add)
+            nc.vector.tensor_tensor(nd[c][:, 1, t, :], ex[t][:].indirect(n2_t[:, lc]), g3, ALU.add)
 
-        def second(c):
-            cols = slice(CH * c, CH * (c + 1))
-            diff, lg = hw[c][:, S : 2 * S], hw[c][:, 2 * S :]
-            nc.scalar.activation(lg, nd[c][:].rearrange("p s t j -> p (s t j)"), ACT.Ln)
-            nc.vector.tensor_tensor(diff, lg[:, :S], lg[:, S:], ALU.subtract)
+        def log_ratio(c, tiles):
+            diff = hw[c][:, S : 2 * S].rearrange("p (t j) -> p t j", t=PACK)
+            lg = hw[c][:, 2 * S :].rearrange("p (s t j) -> p s t j", s=2, t=PACK)
+            nc.scalar.activation(lg[:, :, tiles, :], nd[c][:, :, tiles, :], ACT.Ln)
+            nc.vector.tensor_tensor(diff[:, tiles, :], lg[:, 0, tiles, :], lg[:, 1, tiles, :], ALU.subtract)
+
+        def gain(c):
             z = sb([P, CH, PACK], BF16, "z%d" % c)
             nc.vector.tensor_tensor(
-                z[:], diff.rearrange("p (t j) -> p j t", t=PACK), gn_t[:].unsqueeze(1).to_broadcast([P, CH, PACK]), ALU.mult
+                z[:],
+                hw[c][:, S : 2 * S].rearrange("p (t j) -> p j t", t=PACK),
+                gn_t[:].unsqueeze(1).to_broadcast([P, CH, PACK]),
+                ALU.mult,
             )
+            return z
+
+        def second(c, z):
+            cols = slice(CH * c, CH * (c + 1))
             z_w = sb([P, CH], U32, "z_w%d" % c)
             z_s = sb([P, CH], U8, "z_s%d" % c)
             nc.vector.quantize_mx(out=z_w[:].bitcast(FP8X4), scales=z_s[:], in_=z[:].rearrange("p j t -> p (j t)"))
@@ -170,17 +180,35 @@ def tile_picked_mixhoddsegl_none_po_kernel(
                 product(h_ps[t][:, cols], w3, w3s, t, hz_w[:, cols], hzs[:, cols], True, False)
                 product(h_ps[t][:, cols], w2, w2s, t, z_w[:], z_s[:], False, True)
 
-        for c in range(NCH + 1):
-            if c < NCH:
-                fetch(c)
-            if c > 0:
-                second(c - 1)
+        top_half = sb([P, 1], F32, "top_half")
+        for t in range(PACK):
+            fetch(0, t)
+        for c in range(NCH - 1):
+            fetch(c + 1, 0)
+            fetch(c + 1, 1)
+            log_ratio(c, slice(0, PACK))
+            fetch(c + 1, 2)
+            z = gain(c)
+            fetch(c + 1, 3)
+            second(c, z)
+            if c == 1:
+                nc.vector.tensor_scalar(
+                    hw[0][:, :HALF], h_ps[0][:, :HALF], 1.0, None, ALU.mult, ALU.max, accum_out=top_half[:]
+                )
+        log_ratio(NCH - 1, slice(0, 2))
+        log_ratio(NCH - 1, slice(2, 4))
+        second(NCH - 1, gain(NCH - 1))
 
         ms = sb([P, PACK, S], F32, "ms")
         half_h = sb([P, PACK, S], F32, "half_h")
         for t in range(PACK):
             top = sb([P, 1], F32, "top%d" % t)
-            nc.vector.tensor_scalar(hw[t][:, :S], h_ps[t][:], 1.0, None, ALU.mult, ALU.max, accum_out=top[:])
+            if t == 0:
+                nc.vector.tensor_scalar(
+                    hw[t][:, HALF:S], h_ps[t][:, HALF:], 1.0, top_half[:], ALU.mult, ALU.max, accum_out=top[:]
+                )
+            else:
+                nc.vector.tensor_scalar(hw[t][:, :S], h_ps[t][:], 1.0, None, ALU.mult, ALU.max, accum_out=top[:])
             shift = sb([P, 1], F32, "shift%d" % t)
             nc.vector.tensor_scalar(shift[:], top[:], tau_t[:, t : t + 1], -1.0, ALU.mult, ALU.mult)
             for c in range(2):

@@ -58,7 +58,7 @@ def tile_picked_mixhoddsegl_none_po_kernel(
         nc.sync.dma_start(w_raw[:].bitcast(I32), w1_words[0].bitcast(I32))
         xs_rows = x_scales[0].bitcast(I32).rearrange("(q r) w -> r q w", r=4)
         for r in range(2):
-            nc.sync.dma_start(xs[r:P:32, :].bitcast(I32), xs_rows[r])
+            nc.scalar.dma_start(xs[r:P:32, :].bitcast(I32), xs_rows[r])
         for r in range(2, 4):
             nc.sync.dma_start(xs[r:P:16, :].bitcast(I32), xs_rows[r].unsqueeze(1).to_broadcast([4, 2, T // 4]))
         load_scale_quadrant(nc.sync, ws_raw, w1_scales, 0)
@@ -92,9 +92,8 @@ def tile_picked_mixhoddsegl_none_po_kernel(
             w_raw[:].bitcast(U16).rearrange("p (m t) -> p t m", t=PACK),
         )
         w1s = sb([P, N], U8, "w1s")
-        nc.gpsimd.tensor_copy(
-            w1s[:].rearrange("p (t m) -> p t m", t=PACK), ws_raw[:].rearrange("p (m t) -> p t m", t=PACK)
-        )
+        for t in range(PACK):
+            nc.gpsimd.tensor_copy(w1s[:, P * t : P * (t + 1)], ws_raw[:, t::PACK])
 
         def product(out, w, ws, t, codes, scales, start, stop):
             nc.tensor.matmul_mx(
@@ -136,24 +135,33 @@ def tile_picked_mixhoddsegl_none_po_kernel(
                 v_raw[:, i, :].rearrange("p (m t b) -> p t m b", t=PACK, b=2),
             )
         vs = sb([P, 2, N], U8, "vs")
-        nc.vector.tensor_copy(
-            vs[:].rearrange("p i (t m) -> p i t m", t=PACK), vs_raw[:].rearrange("p i (m t) -> p i t m", t=PACK)
-        )
+        for i in range(2):
+            nc.gpsimd.tensor_copy(
+                vs[:, i, :].rearrange("p (t m) -> p t m", t=PACK), vs_raw[:, i, :].rearrange("p (m t) -> p t m", t=PACK)
+            )
         w2, w2s, w3, w3s = v[:, 0, :], vs[:, 0, :], v[:, 1, :], vs[:, 1, :]
 
         h_ps = [psum.tile([P, S], F32, name="h%d" % t, tag="bank%d" % t) for t in range(PACK)]
-        nd = [sb([P, 2, PACK, CH], F32, "nd%d" % c) for c in range(NCH)]
-        first = [sb([P, PACK, CH], F32, "first%d" % i) for i in range(3)]
-        spaces = [f[:] for f in first] + [nd[c][:, s] for c in range(NCH) for s in range(2)]
+        wide = S - CH
+        sums = sb([P, 2, PACK, wide], F32, "sums")
+        last_sums = sb([P, 2, PACK, CH], F32, "last_sums")
+        nd = [sums[:, :, :, CH * c : CH * (c + 1)] for c in range(NCH - 1)] + [last_sums[:]]
+        for t in range(PACK):
+            got = sb([P, 2, wide], F32, "got%d" % t)
+            nc.scalar.activation(got[:, 0, :], ex[t][:].indirect(n1_t[:, : wide // 16]), ACT.Copy)
+            nc.scalar.activation(got[:, 1, :], ex[t][:].indirect(n3_t[:, : wide // 16]), ACT.Copy)
+            nc.vector.tensor_tensor(sums[:, 0, t, :], ex[t][:, :wide], got[:, 0, :], ALU.add)
+            nc.vector.tensor_tensor(sums[:, 1, t, :], ex[t][:].indirect(n2_t[:, : wide // 16]), got[:, 1, :], ALU.add)
+        g2 = sb([P, PACK, CH], F32, "g2")
+        for t in range(PACK):
+            nc.vector.tensor_copy(g2[:, t, :], ex[t][:].indirect(n2_t[:, wide // 16 :]))
 
-        def fetch(c, t):
-            lc = slice(CH // 16 * c, CH // 16 * (c + 1))
-            space = spaces[2 * c + t // 2]
-            g1, g3 = space[:, 2 * (t % 2), :], space[:, 2 * (t % 2) + 1, :]
-            nc.scalar.activation(g1, ex[t][:].indirect(n1_t[:, lc]), ACT.Copy)
-            nc.scalar.activation(g3, ex[t][:].indirect(n3_t[:, lc]), ACT.Copy)
-            nc.vector.tensor_tensor(nd[c][:, 0, t, :], ex[t][:, CH * c : CH * (c + 1)], g1, ALU.add)
-            nc.vector.tensor_tensor(nd[c][:, 1, t, :], ex[t][:].indirect(n2_t[:, lc]), g3, ALU.add)
+        def fetch_last(t):
+            space = nd[min(t, 2)][:, :, max(t - 2, 0), :]
+            nc.scalar.activation(space[:, 0, :], ex[t][:].indirect(n1_t[:, wide // 16 :]), ACT.Copy)
+            nc.scalar.activation(space[:, 1, :], ex[t][:].indirect(n3_t[:, wide // 16 :]), ACT.Copy)
+            nc.vector.tensor_tensor(last_sums[:, 0, t, :], ex[t][:, wide:], space[:, 0, :], ALU.add)
+            nc.vector.tensor_tensor(last_sums[:, 1, t, :], g2[:, t, :], space[:, 1, :], ALU.add)
 
         def log_ratio(c, tiles):
             diff = hw[c][:, S : 2 * S].rearrange("p (t j) -> p t j", t=PACK)
@@ -181,20 +189,18 @@ def tile_picked_mixhoddsegl_none_po_kernel(
                 product(h_ps[t][:, cols], w2, w2s, t, z_w[:], z_s[:], False, True)
 
         top_half = sb([P, 1], F32, "top_half")
-        for t in range(PACK):
-            fetch(0, t)
-        for c in range(NCH - 1):
-            fetch(c + 1, 0)
-            fetch(c + 1, 1)
+        for c in range(2):
             log_ratio(c, slice(0, PACK))
-            fetch(c + 1, 2)
-            z = gain(c)
-            fetch(c + 1, 3)
-            second(c, z)
-            if c == 1:
-                nc.vector.tensor_scalar(
-                    hw[0][:, :HALF], h_ps[0][:, :HALF], 1.0, None, ALU.mult, ALU.max, accum_out=top_half[:]
-                )
+            second(c, gain(c))
+            fetch_last(c)
+        nc.vector.tensor_scalar(
+            hw[0][:, :HALF], h_ps[0][:, :HALF], 1.0, None, ALU.mult, ALU.max, accum_out=top_half[:]
+        )
+        log_ratio(2, slice(0, PACK))
+        fetch_last(2)
+        z = gain(2)
+        fetch_last(3)
+        second(2, z)
         log_ratio(NCH - 1, slice(0, 2))
         log_ratio(NCH - 1, slice(2, 4))
         second(NCH - 1, gain(NCH - 1))
@@ -235,7 +241,7 @@ def tile_picked_mixhoddsegl_none_po_kernel(
             nc.vector.tensor_tensor(res[:], lm[:], half_h[:, :, cols], ALU.add)
             nc.sync.dma_start(out_rows[:, :, cols], res[:])
             rb = sb([P, CH, PACK], BF16, "rb%d" % c)
-            if c in (1, 2):
+            if c > 0:
                 nc.scalar.copy(rb[:], res[:].rearrange("p t j -> p j t"))
             else:
                 nc.vector.tensor_copy(rb[:], res[:].rearrange("p t j -> p j t"))

from contextlib import ExitStack

import concourse.mybir as mybir

K, T, S, N, H, W = 512, 2048, 512, 512, 512, 2048
FLOPS = 3 * 2 * 512 * 512 * 512

F32 = mybir.dt.float32
BF16 = mybir.dt.bfloat16
I32 = mybir.dt.int32
U32 = mybir.dt.uint32
U16 = mybir.dt.uint16
U8 = mybir.dt.uint8
FP8X4 = mybir.dt.float8_e4m3fn_x4
FP4X4 = mybir.dt.float4_e2m1fn_x4
ACT = mybir.ActivationFunctionType
ALU = mybir.AluOpType
AX = mybir.AxisListType

P = 128
PACK = 4
HALF = S // 2
CH = 128
NCH = S // CH
MEMBERS = 4


def tile_picked_mixhoddsegl_none_po_kernel(
    tc, x_words, x_scales, w1_words, w1_scales, gn, w2_words, w2_scales, w3_words, w3_scales, tau,
    offs, n1, n2, n3, hz, n4, out_0, out_1, out_2,
):
    nc = tc.nc
    with ExitStack() as ctx:
        lists = ctx.enter_context(tc.tile_pool(name="lists", bufs=1))
        keep = ctx.enter_context(tc.tile_pool(name="keep", bufs=1))
        psum = ctx.enter_context(tc.psum_pool(name="psum", bufs=1))

        def sb(shape, dtype, name):
            return keep.tile(shape, dtype, name=name, align_bytes=64)

        def load_list(src, name):
            t = lists.tile(list(src.shape), U16, name=name)
            nc.sync.dma_start(t[:], src)
            return t

        def load_scale_quadrant(queue, dst, src, q):
            queue.dma_start(dst[32 * q : 32 * q + 4, :].bitcast(I32), src[0, 4 * q : 4 * q + 4, :].bitcast(I32))

        w_raw = sb([P, 2 * N], U8, "w_raw")
        ws_raw = sb([P, N], U8, "ws_raw")
        v_raw = sb([P, 2, 2 * N], U8, "v_raw")
        vs_raw = sb([P, 2, N], U8, "vs_raw")

        xs = sb([P, T], U8, "xs")
        nc.gpsimd.memset(xs[:].bitcast(I32), 0)
        nc.vector.memset(ws_raw[:].bitcast(I32), 0)
        offs_t = load_list(offs, "offs_t")
        nc.sync.dma_start(w_raw[:].bitcast(I32), w1_words[0].bitcast(I32))
        xs_rows = x_scales[0].bitcast(I32).rearrange("(q r) w -> r q w", r=4)
        for r in range(2):
            nc.scalar.dma_start(xs[r:P:32, :].bitcast(I32), xs_rows[r])
        for r in range(2, 4):
            nc.sync.dma_start(xs[r:P:16, :].bitcast(I32), xs_rows[r].unsqueeze(1).to_broadcast([4, 2, T // 4]))
        load_scale_quadrant(nc.sync, ws_raw, w1_scales, 0)
        xw = sb([P, T], U32, "xw")
        nc.sync.dma_start(xw[:].bitcast(I32), x_words[0].rearrange("p n t -> p (n t)").bitcast(I32))
        for q in range(1, 4):
            load_scale_quadrant(nc.sync, ws_raw, w1_scales, q)

        nc.vector.memset(vs_raw[:].rearrange("p i n -> p (i n)").bitcast(I32), 0)
        hzs = sb([P, S], U8, "hzs")
        nc.vector.memset(hzs[:].bitcast(I32), 0)
        quarter = sb([P, 1], F32, "quarter")
        nc.vector.memset(quarter[:], 0.25)
        hw = [sb([P, 4 * S], F32, "hw%d" % t) for t in range(PACK)]

        hz_t = load_list(hz, "hz_t")
        n1_t = load_list(n1, "n1_t")
        n3_t = load_list(n3, "n3_t")
        n2_t = load_list(n2, "n2_t")
        gn_t = sb([P, PACK], F32, "gn_t")
        nc.sync.dma_start(gn_t[:], gn.rearrange("(p t) o -> p (t o)", t=PACK))
        for i, words in enumerate((w2_words, w3_words)):
            nc.sync.dma_start(v_raw[:, i, :].bitcast(I32), words[0].bitcast(I32))
        for i, scales in enumerate((w2_scales, w3_scales)):
            for q in range(4):
                load_scale_quadrant(nc.sync, vs_raw[:, i, :], scales, q)

        w1 = sb([P, 2 * N], U8, "w1")
        nc.scalar.copy(
            w1[:].bitcast(U16).rearrange("p (t m) -> p t m", t=PACK),
            w_raw[:].bitcast(U16).rearrange("p (m t) -> p t m", t=PACK),
        )
        w1s = sb([P, N], U8, "w1s")
        for t in range(PACK):
            nc.gpsimd.tensor_copy(w1s[:, P * t : P * (t + 1)], ws_raw[:, t::PACK])

        def product(out, w, ws, t, codes, scales, start, stop):
            nc.tensor.matmul_mx(
                out=out,
                lhsT=w[:, 2 * P * t : 2 * P * (t + 1)].bitcast(FP4X4),
                lhsT_scale=ws[:, P * t : P * (t + 1)],
                rhs=codes.bitcast(FP8X4),
                rhs_scale=scales,
                start=start,
                stop=stop,
            )

        xq_s = sb([P, S], U8, "xq_s")
        nc.vector.tensor_copy(xq_s[:], xs[:].indirect(offs_t[:]))
        ex = [sb([P, S], F32, "ex%d" % t) for t in range(PACK)]
        for u in range(2):
            cols = slice(HALF * u, HALF * (u + 1))
            xq_w = sb([P, HALF], U32, "xq_w%d" % u)
            nc.vector.tensor_copy(xq_w[:], xw[:].indirect(offs_t[:, 16 * u : 16 * (u + 1)]))
            for t in range(PACK):
                y = psum.tile([P, HALF], F32, name="y%d_%d" % (u, t), tag="bank%d" % (4 * u + t))
                product(y[:], w1, w1s, t, xq_w[:], xq_s[:, cols], True, True)
                nc.scalar.activation(ex[t][:, cols], y[:], ACT.Exp, scale=0.5)

        hz_w = sb([P, S], U32, "hz_w")
        nc.vector.tensor_copy(hz_w[:], xw[:].indirect(hz_t[:]))
        hz_s_raw = sb([P, S], U8, "hz_s_raw")
        nc.vector.tensor_copy(hz_s_raw[:], xs[:].indirect(hz_t[:]))
        for r in range(4):
            first = r if r < 2 else 16 + r
            nc.sync.dma_start(hzs[r:P:32, :].bitcast(I32), hz_s_raw[first:P:32, :].bitcast(I32))
        n4_t = load_list(n4, "n4_t")
        tau_t = sb([P, PACK], F32, "tau_t")
        nc.sync.dma_start(tau_t[:], tau.rearrange("(p t) o -> p (t o)", t=PACK))
        v = sb([P, 2, 2 * N], U8, "v")
        for i in range(2):
            nc.gpsimd.tensor_copy(
                v[:, i, :].rearrange("p (t m b) -> p t m b", t=PACK, b=2),
                v_raw[:, i, :].rearrange("p (m t b) -> p t m b", t=PACK, b=2),
            )
        vs = sb([P, 2, N], U8, "vs")
        for i in range(2):
            nc.gpsimd.tensor_copy(
                vs[:, i, :].rearrange("p (t m) -> p t m", t=PACK), vs_raw[:, i, :].rearrange("p (m t) -> p t m", t=PACK)
            )
        w2, w2s, w3, w3s = v[:, 0, :], vs[:, 0, :], v[:, 1, :], vs[:, 1, :]

        h_ps = [psum.tile([P, S], F32, name="h%d" % t, tag="bank%d" % t) for t in range(PACK)]
        wide = S - CH
        sums = sb([P, 2, PACK, wide], F32, "sums")
        last_sums = sb([P, 2, PACK, CH], F32, "last_sums")
        nd = [sums[:, :, :, CH * c : CH * (c + 1)] for c in range(NCH - 1)] + [last_sums[:]]
        for t in range(PACK):
            got = sb([P, 2, wide], F32, "got%d" % t)
            nc.scalar.activation(got[:, 0, :], ex[t][:].indirect(n1_t[:, : wide // 16]), ACT.Copy)
            nc.scalar.activation(got[:, 1, :], ex[t][:].indirect(n3_t[:, : wide // 16]), ACT.Copy)
            nc.vector.tensor_tensor(sums[:, 0, t, :], ex[t][:, :wide], got[:, 0, :], ALU.add)
            nc.vector.tensor_tensor(sums[:, 1, t, :], ex[t][:].indirect(n2_t[:, : wide // 16]), got[:, 1, :], ALU.add)
        g2 = sb([P, PACK, CH], F32, "g2")
        for t in range(PACK):
            nc.vector.tensor_copy(g2[:, t, :], ex[t][:].indirect(n2_t[:, wide // 16 :]))

        def fetch_last(t):
            space = nd[min(t, 2)][:, :, max(t - 2, 0), :]
            nc.scalar.activation(space[:, 0, :], ex[t][:].indirect(n1_t[:, wide // 16 :]), ACT.Copy)
            nc.scalar.activation(space[:, 1, :], ex[t][:].indirect(n3_t[:, wide // 16 :]), ACT.Copy)
            nc.vector.tensor_tensor(last_sums[:, 0, t, :], ex[t][:, wide:], space[:, 0, :], ALU.add)
            nc.vector.tensor_tensor(last_sums[:, 1, t, :], g2[:, t, :], space[:, 1, :], ALU.add)

        def log_ratio(c, tiles):
            diff = hw[c][:, S : 2 * S].rearrange("p (t j) -> p t j", t=PACK)
            lg = hw[c][:, 2 * S :].rearrange("p (s t j) -> p s t j", s=2, t=PACK)
            nc.scalar.activation(lg[:, :, tiles, :], nd[c][:, :, tiles, :], ACT.Ln)
            nc.vector.tensor_tensor(diff[:, tiles, :], lg[:, 0, tiles, :], lg[:, 1, tiles, :], ALU.subtract)

        def gain(c):
            z = sb([P, CH, PACK], BF16, "z%d" % c)
            nc.vector.tensor_tensor(
                z[:],
                hw[c][:, S : 2 * S].rearrange("p (t j) -> p j t", t=PACK),
                gn_t[:].unsqueeze(1).to_broadcast([P, CH, PACK]),
                ALU.mult,
            )
            return z

        def second(c, z):
            cols = slice(CH * c, CH * (c + 1))
            z_w = sb([P, CH], U32, "z_w%d" % c)
            z_s = sb([P, CH], U8, "z_s%d" % c)
            nc.vector.quantize_mx(out=z_w[:].bitcast(FP8X4), scales=z_s[:], in_=z[:].rearrange("p j t -> p (j t)"))
            for t in range(PACK):
                product(h_ps[t][:, cols], w3, w3s, t, hz_w[:, cols], hzs[:, cols], True, False)
                product(h_ps[t][:, cols], w2, w2s, t, z_w[:], z_s[:], False, True)

        top_half = sb([P, 1], F32, "top_half")
        for c in range(2):
            log_ratio(c, slice(0, PACK))
            second(c, gain(c))
            fetch_last(c)
        nc.vector.tensor_scalar(
            hw[0][:, :HALF], h_ps[0][:, :HALF], 1.0, None, ALU.mult, ALU.max, accum_out=top_half[:]
        )
        log_ratio(2, slice(0, PACK))
        fetch_last(2)
        z = gain(2)
        fetch_last(3)
        second(2, z)
        log_ratio(NCH - 1, slice(0, 2))
        log_ratio(NCH - 1, slice(2, 4))
        second(NCH - 1, gain(NCH - 1))

        ms = sb([P, PACK, S], F32, "ms")
        half_h = sb([P, PACK, S], F32, "half_h")
        for t in range(PACK):
            top = sb([P, 1], F32, "top%d" % t)
            if t == 0:
                nc.vector.tensor_scalar(
                    hw[t][:, HALF:S], h_ps[t][:, HALF:], 1.0, top_half[:], ALU.mult, ALU.max, accum_out=top[:]
                )
            else:
                nc.vector.tensor_scalar(hw[t][:, :S], h_ps[t][:], 1.0, None, ALU.mult, ALU.max, accum_out=top[:])
            shift = sb([P, 1], F32, "shift%d" % t)
            nc.vector.tensor_scalar(shift[:], top[:], tau_t[:, t : t + 1], -1.0, ALU.mult, ALU.mult)
            for c in range(2):
                ea = sb([P, HALF, MEMBERS], F32, "ea%d_%d" % (t, c))
                nc.scalar.activation(
                    ea[:].rearrange("p j m -> p (j m)"),
                    hw[t][:].indirect(n4_t[:, 64 * c : 64 * (c + 1)]),
                    ACT.Exp,
                    bias=shift[:],
                    scale=tau_t[:, t : t + 1],
                )
                nc.vector.tensor_reduce(ms[:, t, HALF * c : HALF * (c + 1)], ea[:], AX.X, ALU.add)
            nc.vector.tensor_scalar(half_h[:, t, :], hw[t][:, :S], -0.5, None, ALU.mult)

        out_rows = out_0.rearrange("(p t) j -> p t j", t=PACK)
        out_words = out_1[0].rearrange("p n t -> p (n t)").bitcast(I32)
        o_w = sb([P, S], U32, "o_w")
        o_s = sb([P, S], U8, "o_s")
        for c in range(NCH):
            cols = slice(CH * c, CH * (c + 1))
            lm = sb([P, PACK, CH], F32, "lm%d" % c)
            nc.scalar.activation(lm[:], ms[:, :, cols], ACT.Ln, bias=quarter[:])
            res = sb([P, PACK, CH], F32, "res%d" % c)
            nc.vector.tensor_tensor(res[:], lm[:], half_h[:, :, cols], ALU.add)
            nc.sync.dma_start(out_rows[:, :, cols], res[:])
            rb = sb([P, CH, PACK], BF16, "rb%d" % c)
            if c > 0:
                nc.scalar.copy(rb[:], res[:].rearrange("p t j -> p j t"))
            else:
                nc.vector.tensor_copy(rb[:], res[:].rearrange("p t j -> p j t"))
            nc.vector.quantize_mx(
                out=o_w[:, cols].bitcast(FP8X4), scales=o_s[:, cols], in_=rb[:].rearrange("p j t -> p (j t)")
            )
            nc.sync.dma_start(out_words[:, cols], o_w[:, cols].bitcast(I32))
        for q in range(4):
            queue = nc.sync if q % 2 == 0 else nc.scalar
            queue.dma_start(out_2[0, 4 * q : 4 * q + 4, :].bitcast(I32), o_s[32 * q : 32 * q + 4, :].bitcast(I32))
